import numpy as np
import ml_dtypes


def mxq(x, axis, fmt="e4m3"):
    dtype, down = {"e4m3": (ml_dtypes.float8_e4m3fn, 7), "e5m2": (ml_dtypes.float8_e5m2, 14)}[fmt]
    v = np.moveaxis(np.asarray(x, np.float32).astype(ml_dtypes.bfloat16).astype(np.float64), axis, -1)
    blocks = v.reshape(v.shape[:-1] + (-1, 32))
    amax = np.abs(blocks).max(-1, keepdims=True)
    byte = np.maximum(np.where(amax > 0, np.frexp(amax)[1] - 1 + 127, 0) - down, 1)
    scale = np.exp2(byte - 127.0)
    codes = (blocks / scale).astype(np.float32).astype(dtype).astype(np.float64)
    return np.moveaxis((codes * scale).reshape(v.shape), -1, axis)


WIDE = False


def mx_kscale(k):
    if not WIDE:
        return np.ones(k)
    levels = np.array([30, -30])
    if k % 512:
        return np.exp2(np.random.permutation(np.resize(levels, k // 32))).repeat(32)
    a = np.empty((k // 512, 16))
    for p in range(k // 512):
        a[p, :8] = np.random.permutation(np.resize(levels, 8))
        for g in range(8):
            far = levels[np.abs(levels - a[p, g]) >= 10]
            a[p, g + 8] = far[np.random.randint(len(far))]
    return np.exp2(a.ravel()).repeat(32)


def f64(x):
    return np.asarray(x).astype(np.float64)


def striped(idx):
    return np.tile(np.asarray(idx).reshape(-1, 16).T, (8, 1)).astype(np.uint16)


def unstriped(offs):
    return offs[:16].T.reshape(-1).astype(np.int64)


E2M1 = np.array([0.0, 0.5, 1.0, 1.5, 2.0, 3.0, 4.0, 6.0, -0.0, -0.5, -1.0, -1.5, -2.0, -3.0, -4.0, -6.0])


def pack_weight(w, fmt):
    k, n = w.shape
    w = f64(np.asarray(w, np.float32).astype(ml_dtypes.bfloat16)).reshape(k // 32, 32, n)
    amax = np.abs(w).max(1)
    if fmt == "e4m3":
        byte = np.frexp(amax)[1] - 1 + 127 - 7
    else:
        mant, ex = np.frexp(amax / 6.0)
        byte = np.where(mant > 0.5, ex, ex - 1) + 127
    byte = np.clip(np.where(amax > 0, byte, 1), 1, 254)
    scaled = (w * np.exp2(127.0 - byte)[:, None, :]).reshape(k, n).astype(np.float32)
    by_word = np.ascontiguousarray(scaled.reshape(k // 512, 128, 4, n).transpose(0, 1, 3, 2))
    if fmt == "e4m3":
        words = by_word.astype(ml_dtypes.float8_e4m3fn).view(np.uint8)
    else:
        c = by_word.astype(ml_dtypes.float4_e2m1fn).view(np.uint8) & 0xF
        words = (c[..., 0::2] | (c[..., 1::2] << 4)).reshape(k // 512, 128, 2 * n)
    return np.ascontiguousarray(words), np.ascontiguousarray(byte.astype(np.uint8).reshape(k // 512, 16, n))


def unpack_weight(words, scales, fmt):
    g, _, n = scales.shape
    words = np.ascontiguousarray(words).reshape(g, 128, n, -1)
    if fmt == "e4m3":
        vals = words.view(ml_dtypes.float8_e4m3fn).astype(np.float64)
    else:
        nib = np.empty((g, 128, n, 4), np.uint8)
        nib[..., 0::2] = words & 0xF
        nib[..., 1::2] = words >> 4
        vals = E2M1[nib]
    vals = vals * np.repeat(np.exp2(scales.astype(np.float64) - 127.0), 8, axis=1)[..., None]
    return vals.transpose(0, 1, 3, 2).reshape(g * 512, n)


K, T, J, N = 1024, 1024, 256, 256


def setup_inputs():
    n = np.random.standard_normal
    idx = np.random.permutation(T)[:J]
    idx2 = np.random.permutation(T)[:J]
    fk = mx_kscale(K)
    xtp = pack_weight(n((K, T)) * np.random.uniform(0.4, 1.6, (1, T)) / fk[:, None], "e2m1")
    wap = pack_weight(n((K, N)) * 1 / np.sqrt(K) * fk[:, None], "e2m1")
    return {
        "xt_words": xtp[0],
        "xt_scales": xtp[1],
        "wa_words": wap[0],
        "wa_scales": wap[1],
        "wb": (n((K, N)) * 1 / np.sqrt(K) * fk[:, None]).astype(np.float32),
        "bi": (np.random.uniform(-0.6, 0.6, (1, N))).astype(np.float32),
        "offs": striped(idx),
        "offs2": striped(idx2),
    }


def reference(xt_words, xt_scales, wa_words, wa_scales, wb, bi, offs, offs2):
    idx = unstriped(offs)
    idx2 = unstriped(offs2)
    xtu = unpack_weight(xt_words, xt_scales, "e2m1")
    wau = unpack_weight(wa_words, wa_scales, "e2m1")
    xtidxg = xtu[:, idx]
    a = xtidxg.T @ wau
    xtidx2g = xtu[:, idx2]
    wbq = mxq(f64(wb), 0, "e5m2")
    b0 = xtidx2g.T @ wbq
    b2 = b0 + f64(bi)
    pa = np.max(np.abs(a), axis=1, keepdims=True)
    pb = np.max(np.abs(b2), axis=1, keepdims=True)
    y = 0.3 * (a * pb - b2 * pa)
    return y

@@ -1,0 +1,154 @@
+from contextlib import ExitStack
+
+import concourse.mybir as mybir
+from concourse.masks import make_identity
+
+K, T, J, N = 1024, 1024, 256, 256
+FLOPS = 2 * 2 * J * K * N
+
+F32 = mybir.dt.float32
+BF16 = mybir.dt.bfloat16
+I32 = mybir.dt.int32
+U32 = mybir.dt.uint32
+U16 = mybir.dt.uint16
+U8 = mybir.dt.uint8
+FP4X4 = mybir.dt.float4_e2m1fn_x4
+E5M2X4 = mybir.dt.float8_e5m2_x4
+ALU = mybir.AluOpType
+COPY = mybir.ActivationFunctionType.Copy
+AXIS_X = mybir.AxisListType.X
+
+P = 128
+PACK = 4
+PASSES = K // (P * PACK)
+TILES = J // P
+
+
+def tile_list_rows_twotokens_crosspeaks_kernel(tc, xt_words, xt_scales, wa_words, wa_scales, wb, bi, offs, offs2, out):
+    nc = tc.nc
+    with ExitStack() as ctx:
+        keep = ctx.enter_context(tc.tile_pool(name="keep", bufs=1))
+        psum = ctx.enter_context(tc.psum_pool(name="psum", bufs=1))
+
+        list_a = keep.tile([P, J // 16], U16, name="list_a")
+        list_b = keep.tile([P, J // 16], U16, name="list_b")
+        x_scales = keep.tile([P, T], U8, name="x_scales", align_bytes=64)
+        x_words = [keep.tile([P, T], U16, name=f"x_words{z}", align_bytes=64) for z in range(PASSES)]
+        wb_raw = [keep.tile([P, PACK, N], F32, name=f"wb_raw{z}") for z in range(PASSES)]
+        wa_codes = keep.tile([P, PASSES, 2 * N], U8, name="wa_codes", align_bytes=64)
+        wa_planes = keep.tile([P, PASSES, N], U8, name="wa_planes", align_bytes=64)
+        bias = keep.tile([P, N], F32, name="bias")
+
+        nc.gpsimd.memset(x_scales[:].bitcast(I32), 0)
+        nc.gpsimd.memset(wa_planes[:].rearrange("p z n -> p (z n)").bitcast(I32), 0)
+
+        nc.sync.dma_start(list_b[:], offs2)
+        nc.sync.dma_start(list_a[:], offs)
+        for q in range(4):
+            nc.sync.dma_start(
+                x_scales[32 * q : 32 * q + 8, :].bitcast(I32),
+                xt_scales[:, 4 * q : 4 * q + 4, :].bitcast(I32),
+            )
+        nc.sync.dma_start(x_words[0][:].bitcast(I32), xt_words[0].bitcast(I32))
+        nc.sync.dma_start(wb_raw[0][:], wb[0:512, :].rearrange("(p i) n -> p i n", i=PACK))
+        nc.sync.dma_start(wb_raw[1][:], wb[512:1024, :].rearrange("(p i) n -> p i n", i=PACK))
+        nc.sync.dma_start(x_words[1][:].bitcast(I32), xt_words[1].bitcast(I32))
+        nc.sync.dma_start(wa_codes[:].bitcast(I32), wa_words.rearrange("z p c -> p z c").bitcast(I32))
+        for q in range(4):
+            nc.sync.dma_start(
+                wa_planes[32 * q : 32 * q + 4, :, :].bitcast(I32),
+                wa_scales[:, 4 * q : 4 * q + 4, :].rearrange("z r n -> r z n").bitcast(I32),
+            )
+
+        bias_cols = keep.tile([P, N // P], F32, name="bias_cols")
+        with nc.allow_non_contiguous_dma(reason="one bias value a partition"):
+            nc.gpsimd.dma_start(bias_cols[:], bi[0].rearrange("(c p) -> p c", p=P))
+        identity = keep.tile([P, P], F32, name="identity")
+        make_identity(nc, identity[:])
+        bias_bank = psum.tile([P, N], F32, name="bias_bank")
+        for c in range(N // P):
+            nc.tensor.transpose(bias_bank[:, P * c : P * (c + 1)], bias_cols[:, c : c + 1].to_broadcast([P, P]), identity[:])
+        nc.scalar.copy(bias[:], bias_bank[:])
+
+        def gather_scales(offsets, side):
+            picked = keep.tile([P, J], U8, name=f"scales_{side}0", align_bytes=64)
+            moved = keep.tile([P, J], U8, name=f"scales_{side}1", align_bytes=64)
+            nc.gpsimd.memset(moved[:].bitcast(I32), 0)
+            nc.vector.tensor_copy(picked[:], x_scales[:].indirect(offsets[:]))
+            nc.gpsimd.dma_start(moved[0 : P - 4, :].bitcast(I32), picked[4:P, :].bitcast(I32))
+            return [picked, moved]
+
+        def gather_words(offsets, side, z):
+            picked = keep.tile([P, J], U16, name=f"words_{side}{z}", align_bytes=64)
+            nc.vector.tensor_copy(picked[:], x_words[z][:].indirect(offsets[:]))
+            return picked
+
+        def round_wb(z):
+            grouped = keep.tile([P, N, PACK], BF16, name=f"wb_grouped{z}", align_bytes=64)
+            nc.scalar.copy(
+                grouped[:].rearrange("p (c e) i -> p c i e", e=4),
+                wb_raw[z][:].rearrange("p i (c e) -> p c i e", e=4),
+            )
+            return grouped
+
+        def quantize_wb(grouped, z):
+            codes = keep.tile([P, N], U32, name=f"wb_codes{z}", align_bytes=64)
+            plane = keep.tile([P, N], U8, name=f"wb_plane{z}", align_bytes=64)
+            nc.vector.quantize_mx(out=codes[:].bitcast(E5M2X4), scales=plane[:], in_=grouped[:].rearrange("p n i -> p (n i)"))
+            return codes, plane
+
+        grouped = [round_wb(z) for z in range(PASSES)]
+        scales_b = gather_scales(list_b, "b")
+        scales_a = gather_scales(list_a, "a")
+        words_b = [gather_words(list_b, "b", 0)]
+        words_a = [gather_words(list_a, "a", 0)]
+        wb_q = [quantize_wb(grouped[0], 0)]
+        words_a.append(gather_words(list_a, "a", 1))
+        words_b.append(gather_words(list_b, "b", 1))
+        wb_q.append(quantize_wb(grouped[1], 1))
+
+        acc_a = [psum.tile([P, N], F32, name=f"acc_a{h}") for h in range(TILES)]
+        acc_b = [psum.tile([P, N], F32, name=f"acc_b{h}") for h in range(TILES)]
+
+        def multiply(acc, z, words, scales, moving, moving_plane):
+            for h in range(TILES):
+                cols = slice(P * h, P * (h + 1))
+                nc.tensor.matmul_mx(
+                    out=acc[h][:],
+                    lhsT=words[z][:, cols].bitcast(FP4X4),
+                    lhsT_scale=scales[z][:, cols],
+                    rhs=moving,
+                    rhs_scale=moving_plane,
+                    start=(z == 0),
+                    stop=(z == PASSES - 1),
+                )
+
+        def multiply_a(z):
+            multiply(acc_a, z, words_a, scales_a, wa_codes[:, z, :].bitcast(FP4X4), wa_planes[:, z, :])
+
+        def multiply_b(z):
+            multiply(acc_b, z, words_b, scales_b, wb_q[z][0][:].bitcast(E5M2X4), wb_q[z][1][:])
+
+        multiply_b(0)
+        multiply_a(0)
+        multiply_a(1)
+        multiply_b(1)
+
+        a3 = [keep.tile([P, N], F32, name=f"a3_{h}") for h in range(TILES)]
+        b2 = [keep.tile([P, N], F32, name=f"b2_{h}") for h in range(TILES)]
+        cross = [keep.tile([P, N], F32, name=f"cross{h}") for h in range(TILES)]
+        y = [keep.tile([P, N], F32, name=f"y{h}") for h in range(TILES)]
+        pa3 = [keep.tile([P, 1], F32, name=f"pa3_{h}") for h in range(TILES)]
+        pb = [keep.tile([P, 1], F32, name=f"pb{h}") for h in range(TILES)]
+        for h in range(TILES):
+            nc.scalar.activation(a3[h][:], acc_a[h][:], COPY, scale=0.3)
+        for h in range(TILES):
+            nc.vector.tensor_reduce(pa3[h][:], a3[h][:], AXIS_X, ALU.max, apply_absolute_value=True)
+        for h in range(TILES):
+            nc.vector.tensor_tensor(b2[h][:], acc_b[h][:], bias[:], ALU.add)
+        for h in range(TILES):
+            nc.scalar.activation(cross[h][:], b2[h][:], COPY, scale=pa3[h][:])
+            nc.vector.tensor_reduce(pb[h][:], b2[h][:], AXIS_X, ALU.max, apply_absolute_value=True)
+        for h in range(TILES):
+            nc.vector.scalar_tensor_tensor(y[h][:], a3[h][:], pb[h][:], cross[h][:], ALU.mult, ALU.subtract)
+            nc.sync.dma_start(out[P * h : P * (h + 1), :], y[h][:])

@@ -1,7 +1,6 @@
 from contextlib import ExitStack
 
 import concourse.mybir as mybir
-from concourse.masks import make_identity
 
 K, T, J, N = 1024, 1024, 256, 256
 FLOPS = 2 * 2 * J * K * N
@@ -32,59 +31,56 @@ def tile_list_rows_twotokens_crosspeaks_kernel(tc, xt_words, xt_scales, wa_words
 
         list_a = keep.tile([P, J // 16], U16, name="list_a")
         list_b = keep.tile([P, J // 16], U16, name="list_b")
-        x_scales = keep.tile([P, T], U8, name="x_scales", align_bytes=64)
+        x_scales = keep.tile([P, T], U8, name="x_scales", tag="x_scales", align_bytes=64)
         x_words = [keep.tile([P, T], U16, name=f"x_words{z}", align_bytes=64) for z in range(PASSES)]
         wb_raw = [keep.tile([P, PACK, N], F32, name=f"wb_raw{z}") for z in range(PASSES)]
         wa_codes = keep.tile([P, PASSES, 2 * N], U8, name="wa_codes", align_bytes=64)
         wa_planes = keep.tile([P, PASSES, N], U8, name="wa_planes", align_bytes=64)
-        bias = keep.tile([P, N], F32, name="bias")
 
         nc.gpsimd.memset(x_scales[:].bitcast(I32), 0)
-        nc.gpsimd.memset(wa_planes[:].rearrange("p z n -> p (z n)").bitcast(I32), 0)
+        nc.vector.memset(wa_planes[:].rearrange("p z n -> p (z n)").bitcast(I32), 0)
+
+        nc.gpsimd.dma_start(wa_codes[:].bitcast(I32), wa_words.rearrange("z p c -> p z c").bitcast(I32))
+        bias_seed = keep.tile([P, N], F32, name="bias_seed")
+        bias = keep.tile([P, N], F32, name="bias")
+        nc.gpsimd.dma_start(bias_seed[0:P:8, :], bi[0].partition_broadcast(P // 8))
+        nc.gpsimd.dma_start(bias[:], bias_seed[0:P:8, :].unsqueeze(1).broadcast_to([P // 8, 8, N]))
 
         nc.sync.dma_start(list_b[:], offs2)
+        rows = xt_scales.rearrange("z (a h r) t -> h (z a) r t", h=2, r=4).bitcast(I32)
+        for h in range(2):
+            nc.scalar.dma_start(x_scales[32 * h : 32 * h + 16, :].bitcast(I32), rows[h])
+        for h in range(2):
+            nc.sync.dma_start(x_scales[64 + 32 * h : 68 + 32 * h, :].bitcast(I32), rows[h, 1])
         nc.sync.dma_start(list_a[:], offs)
-        for q in range(4):
-            nc.sync.dma_start(
-                x_scales[32 * q : 32 * q + 8, :].bitcast(I32),
-                xt_scales[:, 4 * q : 4 * q + 4, :].bitcast(I32),
-            )
         nc.sync.dma_start(x_words[0][:].bitcast(I32), xt_words[0].bitcast(I32))
         nc.sync.dma_start(wb_raw[0][:], wb[0:512, :].rearrange("(p i) n -> p i n", i=PACK))
         nc.sync.dma_start(wb_raw[1][:], wb[512:1024, :].rearrange("(p i) n -> p i n", i=PACK))
         nc.sync.dma_start(x_words[1][:].bitcast(I32), xt_words[1].bitcast(I32))
-        nc.sync.dma_start(wa_codes[:].bitcast(I32), wa_words.rearrange("z p c -> p z c").bitcast(I32))
         for q in range(4):
             nc.sync.dma_start(
                 wa_planes[32 * q : 32 * q + 4, :, :].bitcast(I32),
                 wa_scales[:, 4 * q : 4 * q + 4, :].rearrange("z r n -> r z n").bitcast(I32),
             )
 
-        bias_cols = keep.tile([P, N // P], F32, name="bias_cols")
-        with nc.allow_non_contiguous_dma(reason="one bias value a partition"):
-            nc.gpsimd.dma_start(bias_cols[:], bi[0].rearrange("(c p) -> p c", p=P))
-        identity = keep.tile([P, P], F32, name="identity")
-        make_identity(nc, identity[:])
-        bias_bank = psum.tile([P, N], F32, name="bias_bank")
-        for c in range(N // P):
-            nc.tensor.transpose(bias_bank[:, P * c : P * (c + 1)], bias_cols[:, c : c + 1].to_broadcast([P, P]), identity[:])
-        nc.scalar.copy(bias[:], bias_bank[:])
+        picked_scales = keep.tile([P, 2 * J], U8, name="picked_scales", align_bytes=64)
+        moved_scales = keep.tile([P, 2 * J], U8, name="moved_scales", align_bytes=64)
+        nc.vector.tensor_copy(picked_scales[:, 0:J], x_scales[:].indirect(list_b[:]))
+        nc.vector.tensor_copy(picked_scales[:, J : 2 * J], x_scales[:].indirect(list_a[:]))
+        nc.sync.dma_start(moved_scales[0:64, :].bitcast(I32), picked_scales[8:72, :].bitcast(I32))
+        nc.sync.dma_start(moved_scales[64:128, :].bitcast(I32), picked_scales[12:76, :].bitcast(I32))
+        scales_b = [picked_scales[:, 0:J], moved_scales[:, 0:J]]
+        scales_a = [picked_scales[:, J : 2 * J], moved_scales[:, J : 2 * J]]
 
-        def gather_scales(offsets, side):
-            picked = keep.tile([P, J], U8, name=f"scales_{side}0", align_bytes=64)
-            moved = keep.tile([P, J], U8, name=f"scales_{side}1", align_bytes=64)
-            nc.gpsimd.memset(moved[:].bitcast(I32), 0)
-            nc.vector.tensor_copy(picked[:], x_scales[:].indirect(offsets[:]))
-            nc.gpsimd.dma_start(moved[0 : P - 4, :].bitcast(I32), picked[4:P, :].bitcast(I32))
-            return [picked, moved]
-
-        def gather_words(offsets, side, z):
-            picked = keep.tile([P, J], U16, name=f"words_{side}{z}", align_bytes=64)
-            nc.vector.tensor_copy(picked[:], x_words[z][:].indirect(offsets[:]))
-            return picked
+        def gather_words(z, tag, sides):
+            picked = keep.tile([P, 2 * J], U16, name=f"picked_words{z}", tag=tag, align_bytes=64)
+            halves = {"b": picked[:, 0:J], "a": picked[:, J : 2 * J]}
+            for side in sides:
+                nc.vector.tensor_copy(halves[side], x_words[z][:].indirect({"a": list_a, "b": list_b}[side][:]))
+            return halves
 
         def round_wb(z):
-            grouped = keep.tile([P, N, PACK], BF16, name=f"wb_grouped{z}", align_bytes=64)
+            grouped = keep.tile([P, N, PACK], BF16, name=f"wb_grouped{z}", tag=f"wb_grouped{z}", align_bytes=64)
             nc.scalar.copy(
                 grouped[:].rearrange("p (c e) i -> p c i e", e=4),
                 wb_raw[z][:].rearrange("p i (c e) -> p c i e", e=4),
@@ -98,14 +94,12 @@ def tile_list_rows_twotokens_crosspeaks_kernel(tc, xt_words, xt_scales, wa_words
             return codes, plane
 
         grouped = [round_wb(z) for z in range(PASSES)]
-        scales_b = gather_scales(list_b, "b")
-        scales_a = gather_scales(list_a, "a")
-        words_b = [gather_words(list_b, "b", 0)]
-        words_a = [gather_words(list_a, "a", 0)]
+        words = [gather_words(0, "x_scales", "ba")]
         wb_q = [quantize_wb(grouped[0], 0)]
-        words_a.append(gather_words(list_a, "a", 1))
-        words_b.append(gather_words(list_b, "b", 1))
+        words.append(gather_words(1, "wb_grouped0", "ab"))
         wb_q.append(quantize_wb(grouped[1], 1))
+        words_a = [w["a"] for w in words]
+        words_b = [w["b"] for w in words]
 
         acc_a = [psum.tile([P, N], F32, name=f"acc_a{h}") for h in range(TILES)]
         acc_b = [psum.tile([P, N], F32, name=f"acc_b{h}") for h in range(TILES)]

@@ -32,19 +32,17 @@ def tile_list_rows_twotokens_crosspeaks_kernel(tc, xt_words, xt_scales, wa_words
         list_a = keep.tile([P, J // 16], U16, name="list_a")
         list_b = keep.tile([P, J // 16], U16, name="list_b")
         x_scales = keep.tile([P, T], U8, name="x_scales", tag="x_scales", align_bytes=64)
-        x_words = [keep.tile([P, T], U16, name=f"x_words{z}", align_bytes=64) for z in range(PASSES)]
-        wb_raw = [keep.tile([P, PACK, N], F32, name=f"wb_raw{z}") for z in range(PASSES)]
+        x_words = [keep.tile([P, T], U16, name=f"x_words{z}", tag=f"x_words{z}", align_bytes=64) for z in range(PASSES)]
+        wb_raw = [keep.tile([P, PACK, N], F32, name=f"wb_raw{z}", tag=f"wb_raw{z}") for z in range(PASSES)]
         wa_codes = keep.tile([P, PASSES, 2 * N], U8, name="wa_codes", align_bytes=64)
         wa_planes = keep.tile([P, PASSES, N], U8, name="wa_planes", align_bytes=64)
 
         nc.gpsimd.memset(x_scales[:].bitcast(I32), 0)
         nc.vector.memset(wa_planes[:].rearrange("p z n -> p (z n)").bitcast(I32), 0)
 
-        nc.gpsimd.dma_start(wa_codes[:].bitcast(I32), wa_words.rearrange("z p c -> p z c").bitcast(I32))
         bias_seed = keep.tile([P, N], F32, name="bias_seed")
-        bias = keep.tile([P, N], F32, name="bias")
         nc.gpsimd.dma_start(bias_seed[0:P:8, :], bi[0].partition_broadcast(P // 8))
-        nc.gpsimd.dma_start(bias[:], bias_seed[0:P:8, :].unsqueeze(1).broadcast_to([P // 8, 8, N]))
+        nc.gpsimd.dma_start(wa_codes[:].bitcast(I32), wa_words.rearrange("z p c -> p z c").bitcast(I32))
 
         nc.sync.dma_start(list_b[:], offs2)
         rows = xt_scales.rearrange("z (a h r) t -> h (z a) r t", h=2, r=4).bitcast(I32)
@@ -56,12 +54,12 @@ def tile_list_rows_twotokens_crosspeaks_kernel(tc, xt_words, xt_scales, wa_words
         nc.sync.dma_start(x_words[0][:].bitcast(I32), xt_words[0].bitcast(I32))
         nc.sync.dma_start(wb_raw[0][:], wb[0:512, :].rearrange("(p i) n -> p i n", i=PACK))
         nc.sync.dma_start(wb_raw[1][:], wb[512:1024, :].rearrange("(p i) n -> p i n", i=PACK))
-        nc.sync.dma_start(x_words[1][:].bitcast(I32), xt_words[1].bitcast(I32))
         for q in range(4):
             nc.sync.dma_start(
                 wa_planes[32 * q : 32 * q + 4, :, :].bitcast(I32),
                 wa_scales[:, 4 * q : 4 * q + 4, :].rearrange("z r n -> r z n").bitcast(I32),
             )
+        nc.sync.dma_start(x_words[1][:].bitcast(I32), xt_words[1].bitcast(I32))
 
         picked_scales = keep.tile([P, 2 * J], U8, name="picked_scales", align_bytes=64)
         moved_scales = keep.tile([P, 2 * J], U8, name="moved_scales", align_bytes=64)
@@ -88,13 +86,15 @@ def tile_list_rows_twotokens_crosspeaks_kernel(tc, xt_words, xt_scales, wa_words
             return grouped
 
         def quantize_wb(grouped, z):
-            codes = keep.tile([P, N], U32, name=f"wb_codes{z}", align_bytes=64)
+            codes = keep.tile([P, N], U32, name=f"wb_codes{z}", tag=f"x_words{z}", align_bytes=64)
             plane = keep.tile([P, N], U8, name=f"wb_plane{z}", align_bytes=64)
             nc.vector.quantize_mx(out=codes[:].bitcast(E5M2X4), scales=plane[:], in_=grouped[:].rearrange("p n i -> p (n i)"))
             return codes, plane
 
         grouped = [round_wb(z) for z in range(PASSES)]
-        words = [gather_words(0, "x_scales", "ba")]
+        bias = keep.tile([P, N], F32, name="bias", tag="wb_raw0")
+        nc.sync.dma_start(bias[:], bias_seed[0:P:8, :].unsqueeze(1).broadcast_to([P // 8, 8, N]))
+        words = [gather_words(0, "x_scales", "ab")]
         wb_q = [quantize_wb(grouped[0], 0)]
         words.append(gather_words(1, "wb_grouped0", "ab"))
         wb_q.append(quantize_wb(grouped[1], 1))
@@ -123,8 +123,8 @@ def tile_list_rows_twotokens_crosspeaks_kernel(tc, xt_words, xt_scales, wa_words
         def multiply_b(z):
             multiply(acc_b, z, words_b, scales_b, wb_q[z][0][:].bitcast(E5M2X4), wb_q[z][1][:])
 
-        multiply_b(0)
         multiply_a(0)
+        multiply_b(0)
         multiply_a(1)
         multiply_b(1)
 

@@ -18,9 +18,14 @@ COPY = mybir.ActivationFunctionType.Copy
 AXIS_X = mybir.AxisListType.X
 
 P = 128
+HALF = P // 2
+QUAD = 32
+ROWS = 4
 PACK = 4
-PASSES = K // (P * PACK)
+K_PASS = P * PACK
+PASSES = K // K_PASS
 TILES = J // P
+SEED_STEP = 8
 
 
 def tile_list_rows_twotokens_crosspeaks_kernel(tc, xt_words, xt_scales, wa_words, wa_scales, wb, bi, offs, offs2, out):
@@ -33,49 +38,56 @@ def tile_list_rows_twotokens_crosspeaks_kernel(tc, xt_words, xt_scales, wa_words
         list_b = keep.tile([P, J // 16], U16, name="list_b")
         x_scales = keep.tile([P, T], U8, name="x_scales", tag="x_scales", align_bytes=64)
         x_words = [keep.tile([P, T], U16, name=f"x_words{z}", tag=f"x_words{z}", align_bytes=64) for z in range(PASSES)]
-        wb_raw = [keep.tile([P, PACK, N], F32, name=f"wb_raw{z}", tag=f"wb_raw{z}") for z in range(PASSES)]
+        wb_raw = [keep.tile([P, PACK, N], F32, name=f"wb_raw{z}") for z in range(PASSES)]
         wa_codes = keep.tile([P, PASSES, 2 * N], U8, name="wa_codes", align_bytes=64)
         wa_planes = keep.tile([P, PASSES, N], U8, name="wa_planes", align_bytes=64)
+        bias_seed = keep.tile([P, N], F32, name="bias_seed")
 
         nc.gpsimd.memset(x_scales[:].bitcast(I32), 0)
         nc.vector.memset(wa_planes[:].rearrange("p z n -> p (z n)").bitcast(I32), 0)
-
-        bias_seed = keep.tile([P, N], F32, name="bias_seed")
-        nc.gpsimd.dma_start(bias_seed[0:P:8, :], bi[0].partition_broadcast(P // 8))
+        nc.gpsimd.dma_start(bias_seed[0:P:SEED_STEP, :], bi[0].partition_broadcast(P // SEED_STEP))
         nc.gpsimd.dma_start(wa_codes[:].bitcast(I32), wa_words.rearrange("z p c -> p z c").bitcast(I32))
 
+        scale_rows = xt_scales.rearrange("z (u v r) t -> v (z u) r t", v=2, r=ROWS).bitcast(I32)
         nc.sync.dma_start(list_b[:], offs2)
-        rows = xt_scales.rearrange("z (a h r) t -> h (z a) r t", h=2, r=4).bitcast(I32)
-        for h in range(2):
-            nc.scalar.dma_start(x_scales[32 * h : 32 * h + 16, :].bitcast(I32), rows[h])
-        for h in range(2):
-            nc.sync.dma_start(x_scales[64 + 32 * h : 68 + 32 * h, :].bitcast(I32), rows[h, 1])
+        for v in range(2):
+            nc.scalar.dma_start(x_scales[QUAD * v : QUAD * v + 4 * ROWS, :].bitcast(I32), scale_rows[v])
+        for v in range(2):
+            nc.sync.dma_start(x_scales[HALF + QUAD * v : HALF + QUAD * v + ROWS, :].bitcast(I32), scale_rows[v, 1])
         nc.sync.dma_start(list_a[:], offs)
-        nc.sync.dma_start(x_words[0][:].bitcast(I32), xt_words[0].bitcast(I32))
-        nc.sync.dma_start(wb_raw[0][:], wb[0:512, :].rearrange("(p i) n -> p i n", i=PACK))
-        nc.sync.dma_start(wb_raw[1][:], wb[512:1024, :].rearrange("(p i) n -> p i n", i=PACK))
-        for q in range(4):
+
+        def load_x_words(z):
+            nc.sync.dma_start(x_words[z][:].bitcast(I32), xt_words[z].bitcast(I32))
+
+        def load_wb(z):
+            nc.sync.dma_start(wb_raw[z][:], wb[K_PASS * z : K_PASS * (z + 1), :].rearrange("(p i) n -> p i n", i=PACK))
+
+        def load_wa_plane_rows(q):
             nc.sync.dma_start(
-                wa_planes[32 * q : 32 * q + 4, :, :].bitcast(I32),
-                wa_scales[:, 4 * q : 4 * q + 4, :].rearrange("z r n -> r z n").bitcast(I32),
+                wa_planes[QUAD * q : QUAD * q + ROWS, :, :].bitcast(I32),
+                wa_scales[:, ROWS * q : ROWS * (q + 1), :].rearrange("z r n -> r z n").bitcast(I32),
             )
-        nc.sync.dma_start(x_words[1][:].bitcast(I32), xt_words[1].bitcast(I32))
+
+        load_x_words(0)
+        load_wb(0)
+        load_wa_plane_rows(0)
+        load_wb(1)
+        load_x_words(1)
+        for q in range(1, P // QUAD):
+            load_wa_plane_rows(q)
 
         picked_scales = keep.tile([P, 2 * J], U8, name="picked_scales", align_bytes=64)
         moved_scales = keep.tile([P, 2 * J], U8, name="moved_scales", align_bytes=64)
         nc.vector.tensor_copy(picked_scales[:, 0:J], x_scales[:].indirect(list_b[:]))
         nc.vector.tensor_copy(picked_scales[:, J : 2 * J], x_scales[:].indirect(list_a[:]))
-        nc.sync.dma_start(moved_scales[0:64, :].bitcast(I32), picked_scales[8:72, :].bitcast(I32))
-        nc.sync.dma_start(moved_scales[64:128, :].bitcast(I32), picked_scales[12:76, :].bitcast(I32))
+        for u in range(2):
+            first = 2 * ROWS + ROWS * u
+            nc.sync.dma_start(
+                moved_scales[HALF * u : HALF * (u + 1), :].bitcast(I32),
+                picked_scales[first : first + HALF, :].bitcast(I32),
+            )
         scales_b = [picked_scales[:, 0:J], moved_scales[:, 0:J]]
         scales_a = [picked_scales[:, J : 2 * J], moved_scales[:, J : 2 * J]]
-
-        def gather_words(z, tag, sides):
-            picked = keep.tile([P, 2 * J], U16, name=f"picked_words{z}", tag=tag, align_bytes=64)
-            halves = {"b": picked[:, 0:J], "a": picked[:, J : 2 * J]}
-            for side in sides:
-                nc.vector.tensor_copy(halves[side], x_words[z][:].indirect({"a": list_a, "b": list_b}[side][:]))
-            return halves
 
         def round_wb(z):
             grouped = keep.tile([P, N, PACK], BF16, name=f"wb_grouped{z}", tag=f"wb_grouped{z}", align_bytes=64)
@@ -85,64 +97,63 @@ def tile_list_rows_twotokens_crosspeaks_kernel(tc, xt_words, xt_scales, wa_words
             )
             return grouped
 
-        def quantize_wb(grouped, z):
-            codes = keep.tile([P, N], U32, name=f"wb_codes{z}", tag=f"x_words{z}", align_bytes=64)
+        def quantize_wb(grouped, z, tag):
+            codes = keep.tile([P, N], U32, name=f"wb_codes{z}", tag=tag, align_bytes=64)
             plane = keep.tile([P, N], U8, name=f"wb_plane{z}", align_bytes=64)
             nc.vector.quantize_mx(out=codes[:].bitcast(E5M2X4), scales=plane[:], in_=grouped[:].rearrange("p n i -> p (n i)"))
-            return codes, plane
+            return codes[:].bitcast(E5M2X4), plane[:]
 
-        grouped = [round_wb(z) for z in range(PASSES)]
-        bias = keep.tile([P, N], F32, name="bias", tag="wb_raw0")
-        nc.sync.dma_start(bias[:], bias_seed[0:P:8, :].unsqueeze(1).broadcast_to([P // 8, 8, N]))
-        words = [gather_words(0, "x_scales", "ab")]
-        wb_q = [quantize_wb(grouped[0], 0)]
-        words.append(gather_words(1, "wb_grouped0", "ab"))
-        wb_q.append(quantize_wb(grouped[1], 1))
-        words_a = [w["a"] for w in words]
-        words_b = [w["b"] for w in words]
+        def gather_words(picked, z, offsets):
+            nc.vector.tensor_copy(picked, x_words[z][:].indirect(offsets[:]))
+            return picked
+
+        wb_grouped = [round_wb(z) for z in range(PASSES)]
+
+        bias = keep.tile([P, N], F32, name="bias")
+        nc.sync.dma_start(bias[:], bias_seed[0:P:SEED_STEP, :].unsqueeze(1).broadcast_to([P // SEED_STEP, SEED_STEP, N]))
+
+        picked_0 = keep.tile([P, 2 * J], U16, name="picked_0", tag="x_scales", align_bytes=64)
+        words_b = [gather_words(picked_0[:, 0:J], 0, list_b)]
+        words_a = [gather_words(picked_0[:, J : 2 * J], 0, list_a)]
+        wb_quantized = [quantize_wb(wb_grouped[0], 0, "x_words0")]
+        picked_b1 = keep.tile([P, J], U16, name="picked_b1", tag="wb_grouped0", align_bytes=64)
+        words_b.append(gather_words(picked_b1[:], 1, list_b))
+        wb_quantized.append(quantize_wb(wb_grouped[1], 1, "wb_codes1"))
+        picked_a1 = keep.tile([P, J], U16, name="picked_a1", tag="wb_grouped1", align_bytes=64)
+        words_a.append(gather_words(picked_a1[:], 1, list_a))
+        wa_quantized = [(wa_codes[:, z, :].bitcast(FP4X4), wa_planes[:, z, :]) for z in range(PASSES)]
 
         acc_a = [psum.tile([P, N], F32, name=f"acc_a{h}") for h in range(TILES)]
         acc_b = [psum.tile([P, N], F32, name=f"acc_b{h}") for h in range(TILES)]
+        for z in range(PASSES):
+            for acc, words, scales, weight in ((acc_b, words_b, scales_b, wb_quantized), (acc_a, words_a, scales_a, wa_quantized)):
+                for h in range(TILES):
+                    slots = slice(P * h, P * (h + 1))
+                    nc.tensor.matmul_mx(
+                        out=acc[h][:],
+                        lhsT=words[z][:, slots].bitcast(FP4X4),
+                        lhsT_scale=scales[z][:, slots],
+                        rhs=weight[z][0],
+                        rhs_scale=weight[z][1],
+                        start=(z == 0),
+                        stop=(z == PASSES - 1),
+                    )
 
-        def multiply(acc, z, words, scales, moving, moving_plane):
-            for h in range(TILES):
-                cols = slice(P * h, P * (h + 1))
-                nc.tensor.matmul_mx(
-                    out=acc[h][:],
-                    lhsT=words[z][:, cols].bitcast(FP4X4),
-                    lhsT_scale=scales[z][:, cols],
-                    rhs=moving,
-                    rhs_scale=moving_plane,
-                    start=(z == 0),
-                    stop=(z == PASSES - 1),
-                )
-
-        def multiply_a(z):
-            multiply(acc_a, z, words_a, scales_a, wa_codes[:, z, :].bitcast(FP4X4), wa_planes[:, z, :])
-
-        def multiply_b(z):
-            multiply(acc_b, z, words_b, scales_b, wb_q[z][0][:].bitcast(E5M2X4), wb_q[z][1][:])
-
-        multiply_a(0)
-        multiply_b(0)
-        multiply_a(1)
-        multiply_b(1)
-
+        minus_b2 = [keep.tile([P, N], F32, name=f"minus_b2_{h}") for h in range(TILES)]
         a3 = [keep.tile([P, N], F32, name=f"a3_{h}") for h in range(TILES)]
-        b2 = [keep.tile([P, N], F32, name=f"b2_{h}") for h in range(TILES)]
-        cross = [keep.tile([P, N], F32, name=f"cross{h}") for h in range(TILES)]
-        y = [keep.tile([P, N], F32, name=f"y{h}") for h in range(TILES)]
-        pa3 = [keep.tile([P, 1], F32, name=f"pa3_{h}") for h in range(TILES)]
+        a3_pb = [keep.tile([P, N], F32, name=f"a3_pb_{h}") for h in range(TILES)]
+        result = [keep.tile([P, N], F32, name=f"result{h}") for h in range(TILES)]
         pb = [keep.tile([P, 1], F32, name=f"pb{h}") for h in range(TILES)]
+        pa3 = [keep.tile([P, 1], F32, name=f"pa3_{h}") for h in range(TILES)]
+        for h in range(TILES):
+            nc.vector.scalar_tensor_tensor(minus_b2[h][:], acc_b[h][:], -1.0, bias[:], ALU.mult, ALU.subtract)
+        for h in range(TILES):
+            nc.vector.tensor_reduce(pb[h][:], minus_b2[h][:], AXIS_X, ALU.max, apply_absolute_value=True)
         for h in range(TILES):
             nc.scalar.activation(a3[h][:], acc_a[h][:], COPY, scale=0.3)
         for h in range(TILES):
+            nc.scalar.activation(a3_pb[h][:], a3[h][:], COPY, scale=pb[h][:])
             nc.vector.tensor_reduce(pa3[h][:], a3[h][:], AXIS_X, ALU.max, apply_absolute_value=True)
         for h in range(TILES):
-            nc.vector.tensor_tensor(b2[h][:], acc_b[h][:], bias[:], ALU.add)
-        for h in range(TILES):
-            nc.scalar.activation(cross[h][:], b2[h][:], COPY, scale=pa3[h][:])
-            nc.vector.tensor_reduce(pb[h][:], b2[h][:], AXIS_X, ALU.max, apply_absolute_value=True)
-        for h in range(TILES):
-            nc.vector.scalar_tensor_tensor(y[h][:], a3[h][:], pb[h][:], cross[h][:], ALU.mult, ALU.subtract)
-            nc.sync.dma_start(out[P * h : P * (h + 1), :], y[h][:])
+            nc.vector.scalar_tensor_tensor(result[h][:], minus_b2[h][:], pa3[h][:], a3_pb[h][:], ALU.mult, ALU.add)
+            nc.sync.dma_start(out[P * h : P * (h + 1), :], result[h][:])

from contextlib import ExitStack

import concourse.mybir as mybir

K, T, J, N = 1024, 1024, 256, 256
FLOPS = 2 * 2 * J * K * N

F32 = mybir.dt.float32
BF16 = mybir.dt.bfloat16
I32 = mybir.dt.int32
U32 = mybir.dt.uint32
U16 = mybir.dt.uint16
U8 = mybir.dt.uint8
FP4X4 = mybir.dt.float4_e2m1fn_x4
E5M2X4 = mybir.dt.float8_e5m2_x4
ALU = mybir.AluOpType
COPY = mybir.ActivationFunctionType.Copy
AXIS_X = mybir.AxisListType.X

P = 128
HALF = P // 2
QUAD = 32
ROWS = 4
PACK = 4
K_PASS = P * PACK
PASSES = K // K_PASS
TILES = J // P
SEED_STEP = 8


def tile_list_rows_twotokens_crosspeaks_kernel(tc, xt_words, xt_scales, wa_words, wa_scales, wb, bi, offs, offs2, out):
    nc = tc.nc
    with ExitStack() as ctx:
        keep = ctx.enter_context(tc.tile_pool(name="keep", bufs=1))
        psum = ctx.enter_context(tc.psum_pool(name="psum", bufs=1))

        list_a = keep.tile([P, J // 16], U16, name="list_a")
        list_b = keep.tile([P, J // 16], U16, name="list_b")
        x_scales = keep.tile([P, T], U8, name="x_scales", tag="x_scales", align_bytes=64)
        x_words = [keep.tile([P, T], U16, name=f"x_words{z}", tag=f"x_words{z}", align_bytes=64) for z in range(PASSES)]
        wb_raw = [keep.tile([P, PACK, N], F32, name=f"wb_raw{z}") for z in range(PASSES)]
        wa_codes = keep.tile([P, PASSES, 2 * N], U8, name="wa_codes", align_bytes=64)
        wa_planes = keep.tile([P, PASSES, N], U8, name="wa_planes", align_bytes=64)
        bias_seed = keep.tile([P, N], F32, name="bias_seed")

        nc.gpsimd.memset(x_scales[:].bitcast(I32), 0)
        nc.vector.memset(wa_planes[:].rearrange("p z n -> p (z n)").bitcast(I32), 0)
        nc.gpsimd.dma_start(bias_seed[0:P:SEED_STEP, :], bi[0].partition_broadcast(P // SEED_STEP))
        nc.gpsimd.dma_start(wa_codes[:].bitcast(I32), wa_words.rearrange("z p c -> p z c").bitcast(I32))

        scale_rows = xt_scales.rearrange("z (u v r) t -> v (z u) r t", v=2, r=ROWS).bitcast(I32)
        nc.sync.dma_start(list_b[:], offs2)
        for v in range(2):
            nc.scalar.dma_start(x_scales[QUAD * v : QUAD * v + 4 * ROWS, :].bitcast(I32), scale_rows[v])
        for v in range(2):
            nc.sync.dma_start(x_scales[HALF + QUAD * v : HALF + QUAD * v + ROWS, :].bitcast(I32), scale_rows[v, 1])
        nc.sync.dma_start(list_a[:], offs)

        def load_x_words(z):
            nc.sync.dma_start(x_words[z][:].bitcast(I32), xt_words[z].bitcast(I32))

        def load_wb(z):
            nc.sync.dma_start(wb_raw[z][:], wb[K_PASS * z : K_PASS * (z + 1), :].rearrange("(p i) n -> p i n", i=PACK))

        def load_wa_plane_rows(q):
            nc.sync.dma_start(
                wa_planes[QUAD * q : QUAD * q + ROWS, :, :].bitcast(I32),
                wa_scales[:, ROWS * q : ROWS * (q + 1), :].rearrange("z r n -> r z n").bitcast(I32),
            )

        load_x_words(0)
        load_wb(0)
        load_wa_plane_rows(0)
        load_wb(1)
        load_x_words(1)
        for q in range(1, P // QUAD):
            load_wa_plane_rows(q)

        picked_scales = keep.tile([P, 2 * J], U8, name="picked_scales", align_bytes=64)
        moved_scales = keep.tile([P, 2 * J], U8, name="moved_scales", align_bytes=64)
        nc.vector.tensor_copy(picked_scales[:, 0:J], x_scales[:].indirect(list_b[:]))
        nc.vector.tensor_copy(picked_scales[:, J : 2 * J], x_scales[:].indirect(list_a[:]))
        for u in range(2):
            first = 2 * ROWS + ROWS * u
            nc.sync.dma_start(
                moved_scales[HALF * u : HALF * (u + 1), :].bitcast(I32),
                picked_scales[first : first + HALF, :].bitcast(I32),
            )
        scales_b = [picked_scales[:, 0:J], moved_scales[:, 0:J]]
        scales_a = [picked_scales[:, J : 2 * J], moved_scales[:, J : 2 * J]]

        def round_wb(z):
            grouped = keep.tile([P, N, PACK], BF16, name=f"wb_grouped{z}", tag=f"wb_grouped{z}", align_bytes=64)
            nc.scalar.copy(
                grouped[:].rearrange("p (c e) i -> p c i e", e=4),
                wb_raw[z][:].rearrange("p i (c e) -> p c i e", e=4),
            )
            return grouped

        def quantize_wb(grouped, z, tag):
            codes = keep.tile([P, N], U32, name=f"wb_codes{z}", tag=tag, align_bytes=64)
            plane = keep.tile([P, N], U8, name=f"wb_plane{z}", align_bytes=64)
            nc.vector.quantize_mx(out=codes[:].bitcast(E5M2X4), scales=plane[:], in_=grouped[:].rearrange("p n i -> p (n i)"))
            return codes[:].bitcast(E5M2X4), plane[:]

        def gather_words(picked, z, offsets):
            nc.vector.tensor_copy(picked, x_words[z][:].indirect(offsets[:]))
            return picked

        wb_grouped = [round_wb(z) for z in range(PASSES)]

        bias = keep.tile([P, N], F32, name="bias")
        nc.sync.dma_start(bias[:], bias_seed[0:P:SEED_STEP, :].unsqueeze(1).broadcast_to([P // SEED_STEP, SEED_STEP, N]))

        picked_0 = keep.tile([P, 2 * J], U16, name="picked_0", tag="x_scales", align_bytes=64)
        words_b = [gather_words(picked_0[:, 0:J], 0, list_b)]
        words_a = [gather_words(picked_0[:, J : 2 * J], 0, list_a)]
        wb_quantized = [quantize_wb(wb_grouped[0], 0, "x_words0")]
        picked_b1 = keep.tile([P, J], U16, name="picked_b1", tag="wb_grouped0", align_bytes=64)
        words_b.append(gather_words(picked_b1[:], 1, list_b))
        wb_quantized.append(quantize_wb(wb_grouped[1], 1, "wb_codes1"))
        picked_a1 = keep.tile([P, J], U16, name="picked_a1", tag="wb_grouped1", align_bytes=64)
        words_a.append(gather_words(picked_a1[:], 1, list_a))
        wa_quantized = [(wa_codes[:, z, :].bitcast(FP4X4), wa_planes[:, z, :]) for z in range(PASSES)]

        acc_a = [psum.tile([P, N], F32, name=f"acc_a{h}") for h in range(TILES)]
        acc_b = [psum.tile([P, N], F32, name=f"acc_b{h}") for h in range(TILES)]
        for z in range(PASSES):
            for acc, words, scales, weight in ((acc_b, words_b, scales_b, wb_quantized), (acc_a, words_a, scales_a, wa_quantized)):
                for h in range(TILES):
                    slots = slice(P * h, P * (h + 1))
                    nc.tensor.matmul_mx(
                        out=acc[h][:],
                        lhsT=words[z][:, slots].bitcast(FP4X4),
                        lhsT_scale=scales[z][:, slots],
                        rhs=weight[z][0],
                        rhs_scale=weight[z][1],
                        start=(z == 0),
                        stop=(z == PASSES - 1),
                    )

        minus_b2 = [keep.tile([P, N], F32, name=f"minus_b2_{h}") for h in range(TILES)]
        a3 = [keep.tile([P, N], F32, name=f"a3_{h}") for h in range(TILES)]
        a3_pb = [keep.tile([P, N], F32, name=f"a3_pb_{h}") for h in range(TILES)]
        result = [keep.tile([P, N], F32, name=f"result{h}") for h in range(TILES)]
        pb = [keep.tile([P, 1], F32, name=f"pb{h}") for h in range(TILES)]
        pa3 = [keep.tile([P, 1], F32, name=f"pa3_{h}") for h in range(TILES)]
        for h in range(TILES):
            nc.vector.scalar_tensor_tensor(minus_b2[h][:], acc_b[h][:], -1.0, bias[:], ALU.mult, ALU.subtract)
        for h in range(TILES):
            nc.vector.tensor_reduce(pb[h][:], minus_b2[h][:], AXIS_X, ALU.max, apply_absolute_value=True)
        for h in range(TILES):
            nc.scalar.activation(a3[h][:], acc_a[h][:], COPY, scale=0.3)
        for h in range(TILES):
            nc.scalar.activation(a3_pb[h][:], a3[h][:], COPY, scale=pb[h][:])
            nc.vector.tensor_reduce(pa3[h][:], a3[h][:], AXIS_X, ALU.max, apply_absolute_value=True)
        for h in range(TILES):
            nc.vector.scalar_tensor_tensor(result[h][:], minus_b2[h][:], pa3[h][:], a3_pb[h][:], ALU.mult, ALU.add)
            nc.sync.dma_start(out[P * h : P * (h + 1), :], result[h][:])
